import numpy as np
import ml_dtypes


def mxq(x, axis, fmt="e4m3"):
    dtype, down = {"e4m3": (ml_dtypes.float8_e4m3fn, 7), "e5m2": (ml_dtypes.float8_e5m2, 14)}[fmt]
    v = np.moveaxis(np.asarray(x, np.float32).astype(ml_dtypes.bfloat16).astype(np.float64), axis, -1)
    blocks = v.reshape(v.shape[:-1] + (-1, 32))
    amax = np.abs(blocks).max(-1, keepdims=True)
    byte = np.maximum(np.where(amax > 0, np.frexp(amax)[1] - 1 + 127, 0) - down, 1)
    scale = np.exp2(byte - 127.0)
    codes = (blocks / scale).astype(np.float32).astype(dtype).astype(np.float64)
    return np.moveaxis((codes * scale).reshape(v.shape), -1, axis)


WIDE = False


def mx_kscale(k):
    if not WIDE:
        return np.ones(k)
    levels = np.array([10, -10, 5, -5, 0])
    if k % 512:
        return np.exp2(np.random.permutation(np.resize(levels, k // 32))).repeat(32)
    a = np.empty((k // 512, 16))
    for p in range(k // 512):
        a[p, :8] = np.random.permutation(np.resize(levels, 8))
        for g in range(8):
            far = levels[np.abs(levels - a[p, g]) >= 10]
            a[p, g + 8] = far[np.random.randint(len(far))]
    return np.exp2(a.ravel()).repeat(32)


def f64(x):
    return np.asarray(x).astype(np.float64)


def striped(idx):
    return np.tile(idx.reshape(-1, 16).T, (8, 1)).astype(np.uint16)


def unstriped(offs):
    return offs[:16].T.reshape(-1).astype(np.int64)


def striped8(idx):
    return np.concatenate([x.reshape(-1, 16).T for x in idx]).astype(np.uint16)


def runs(offs, k):
    lists = np.stack([offs[16 * r : 16 * r + 16].T.reshape(-1) for r in range(8)]).astype(np.int64)
    return lists[np.arange(k) % 512 // 64]


def pack_weight(w):
    k, n = w.shape
    w = f64(np.asarray(w, np.float32).astype(ml_dtypes.bfloat16)).reshape(k // 32, 32, n)
    amax = np.abs(w).max(1)
    byte = np.clip(np.where(amax > 0, np.frexp(amax)[1] - 1 + 127 - 7, 1), 1, 254)
    scaled = (w * np.exp2(127.0 - byte)[:, None, :]).reshape(k, n).astype(np.float32)
    words = np.ascontiguousarray(scaled.reshape(k // 512, 128, 4, n).transpose(0, 1, 3, 2)).astype(ml_dtypes.float8_e4m3fn).view(np.uint8)
    return words, np.ascontiguousarray(byte.astype(np.uint8).reshape(k // 512, 16, n))


def unpack_weight(words, scales):
    g, p, n, _ = words.shape
    vals = np.ascontiguousarray(words).view(ml_dtypes.float8_e4m3fn).astype(np.float64) * np.repeat(np.exp2(scales.astype(np.float64) - 127.0), 8, axis=1)[..., None]
    return vals.transpose(0, 1, 3, 2).reshape(g * 512, n)


K, T, S, V, H = 512, 2048, 512, 512, 512


def setup_inputs():
    n = np.random.standard_normal
    s = mx_kscale(K)[:, None]
    u = mx_kscale(S)
    packed_xT = pack_weight(n((K, T)) * s)
    return {
        "x_words": packed_xT[0],
        "x_scales": packed_xT[1],
        "w1": (n((K, H)) / np.sqrt(K) / s).astype(np.float32),
        "w2": (n((K, H)) / np.sqrt(K) / s).astype(np.float32),
        "w3": (n((K, H)) / np.sqrt(K) / s).astype(np.float32),
        "ga": (np.random.uniform(0.5, 1.5, (H, 1)) * u[:, None]).astype(np.float32),
        "gb": (np.random.uniform(0.5, 1.5, (H, 1)) / u[:, None]).astype(np.float32),
        "offs": striped(np.random.permutation(T)[:S]),
        "two": striped(np.random.permutation(T)[:S]),
        "n1": striped8(np.stack([np.random.permutation(S) for _ in range(8)])),
        "n2": striped8(np.stack([np.random.permutation(S) for _ in range(8)])),
        "n3": striped8(np.stack([np.random.permutation(S) for _ in range(8)])),
        "three": striped(np.random.permutation(T)[:V]),
        "n4": striped8(np.stack([np.random.permutation(V) for _ in range(8)])),
        "n5": striped8(np.stack([np.random.permutation(V) for _ in range(8)])),
        "n6": striped8(np.stack([np.random.permutation(V) for _ in range(8)])),
    }


def reference(x_words, x_scales, w1, w2, w3, ga, gb, offs, two, n1, n2, n3, three, n4, n5, n6):
    xq = unpack_weight(x_words, x_scales)[:, unstriped(offs)]
    y = mxq(f64(w1), 0, "e4m3").T @ xq
    x_two = unpack_weight(x_words, x_scales)[:, unstriped(two)]
    d = mxq(f64(w2), 0, "e4m3").T @ x_two
    z = f64(ga) * (np.maximum(np.minimum(y - (0.5 * (y[np.arange(H)[:, None], runs(n1, H)])), d[np.arange(H)[:, None], runs(n2, H)]), d[np.arange(H)[:, None], runs(n3, H)]))
    x_three = unpack_weight(x_words, x_scales)[:, unstriped(three)]
    b = mxq(f64(w3), 0, "e4m3").T @ x_three
    z2 = f64(gb) * (b / (np.abs(b[np.arange(H)[:, None], runs(n4, H)]) + 0.5))
    s = 0.0625 * ((mxq(z, 0, "e4m3").T @ mxq(z2, 0, "e4m3")))
    return s[np.arange(S)[:, None], runs(n5, S)] - (s[np.arange(S)[:, None], runs(n6, S)])

@@ -1,0 +1,201 @@
+from contextlib import ExitStack
+
+import concourse.mybir as mybir
+
+F32 = mybir.dt.float32
+BF16 = mybir.dt.bfloat16
+I32 = mybir.dt.int32
+U32 = mybir.dt.uint32
+U16 = mybir.dt.uint16
+U8 = mybir.dt.uint8
+FP8X4 = mybir.dt.float8_e4m3fn_x4
+ALU = mybir.AluOpType
+ACT = mybir.ActivationFunctionType
+
+P = 128
+T = 2048
+N = 512
+PACK = 4
+FLOPS = 4 * 2 * 512 * 512 * 512
+
+
+def tile_picked_twkclampbnormgap_none_p_kernel(
+    tc, x_words, x_scales, w1, w2, w3, ga, gb, offs, two, n1, n2, n3, three, n4, n5, n6, out
+):
+    nc = tc.nc
+    with ExitStack() as ctx:
+        keep = ctx.enter_context(tc.tile_pool(name="keep", bufs=1))
+        ring = ctx.enter_context(tc.tile_pool(name="ring", bufs=4))
+        psum = ctx.enter_context(tc.psum_pool(name="psum", bufs=8))
+
+        def load_list(name, src):
+            tile = keep.tile([P, N // 16], U16, name=name)
+            nc.sync.dma_start(tile[:], src)
+            return tile
+
+        def load_weight(name, src):
+            tile = keep.tile([P, PACK, N], F32, name=name)
+            nc.sync.dma_start(tile[:], src.rearrange("(p j) c -> p j c", j=PACK))
+            return tile
+
+        x_bytes = keep.tile([P, T], U8, name="x_bytes")
+        nc.vector.memset(x_bytes[:].bitcast(I32), 0)
+        half = keep.tile([P, 1], F32, name="half")
+        nc.vector.memset(half[:], 0.5)
+        warm = keep.tile([P, 1], F32, name="warm")
+        nc.scalar.activation(warm[:], half[:], ACT.Ln)
+
+        l_offs = load_list("l_offs", offs)
+        x_table = keep.tile([P, T], I32, name="x_table")
+        nc.sync.dma_start(x_table[:], x_words[0].rearrange("p n t -> p (n t)").bitcast(I32))
+        for q in range(4):
+            nc.sync.dma_start(
+                x_bytes[32 * q : 32 * q + 4, :].bitcast(I32), x_scales[0, 4 * q : 4 * q + 4, :].bitcast(I32)
+            )
+        w1_raw = load_weight("w1_raw", w1)
+        l_two = load_list("l_two", two)
+        l_three = load_list("l_three", three)
+        w2_raw = load_weight("w2_raw", w2)
+        l_n1 = load_list("l_n1", n1)
+        w3_raw = load_weight("w3_raw", w3)
+        l_n2 = load_list("l_n2", n2)
+        l_n3 = load_list("l_n3", n3)
+        l_n4 = load_list("l_n4", n4)
+        l_n6 = load_list("l_n6", n6)
+        l_n5 = load_list("l_n5", n5)
+
+        ga_t = keep.tile([P, PACK], F32, name="ga_t")
+        gb_t = keep.tile([P, PACK], F32, name="gb_t")
+        nc.gpsimd.dma_start(ga_t[:], ga.rearrange("(p t) o -> p (t o)", t=PACK))
+        nc.gpsimd.dma_start(gb_t[:], gb.rearrange("(p t) o -> p (t o)", t=PACK))
+        step = keep.tile([P, PACK], F32, name="step")
+        sgn = keep.tile([P, PACK], F32, name="sgn")
+        ga_abs = keep.tile([P, PACK], F32, name="ga_abs")
+        gb_sgn = keep.tile([P, PACK], F32, name="gb_sgn")
+        nc.gpsimd.tensor_scalar(step[:], ga_t[:], 0.0, 2.0, ALU.is_ge, ALU.mult)
+        nc.gpsimd.tensor_scalar(sgn[:], step[:], 1.0, -1.0, ALU.mult, ALU.add)
+        nc.gpsimd.tensor_tensor(ga_abs[:], ga_t[:], sgn[:], ALU.mult)
+        nc.gpsimd.tensor_tensor(gb_sgn[:], gb_t[:], sgn[:], ALU.mult)
+
+        win_a = [keep.tile([P, 2 * N], F32, name="win_a%d" % t) for t in range(PACK)]
+        win_b = [keep.tile([P, 2 * N], F32, name="win_b%d" % t) for t in range(PACK)]
+        for win in win_a + win_b:
+            nc.vector.memset(win[:, N:], 0.0)
+
+        def pick(name, offsets, tag):
+            words = keep.tile([P, N], U32, name=name + "_words", tag=tag, align_bytes=64)
+            scales = keep.tile([P, N], U8, name=name + "_scales", align_bytes=64)
+            nc.vector.tensor_copy(words[:], x_table[:].bitcast(U32).indirect(offsets[:]))
+            nc.vector.tensor_copy(scales[:], x_bytes[:].indirect(offsets[:]))
+            return words, scales
+
+        def quantise(name, rounded, width):
+            words = keep.tile([P, width], U32, name=name + "_words", align_bytes=64)
+            scales = keep.tile([P, width], U8, name=name + "_scales", align_bytes=64)
+            nc.vector.quantize_mx(out=words[:].bitcast(FP8X4), scales=scales[:], in_=rounded[:])
+            return words, scales
+
+        def round_weight(name, raw, copy):
+            rounded = keep.tile([P, PACK * N], BF16, name=name, align_bytes=64)
+            copy(
+                rounded[:].rearrange("p (t m j) -> p m j t", t=PACK, j=PACK),
+                raw[:].rearrange("p j (m t) -> p m j t", t=PACK),
+            )
+            return rounded
+
+        def product(stationary, tile_index, moving):
+            acc = psum.tile([P, N], F32, name="acc")
+            cols = slice(tile_index * P, (tile_index + 1) * P)
+            nc.tensor.matmul_mx(
+                out=acc[:],
+                lhsT=stationary[0][:, cols].bitcast(FP8X4),
+                lhsT_scale=stationary[1][:, cols],
+                rhs=moving[0][:].bitcast(FP8X4),
+                rhs_scale=moving[1][:],
+                start=True,
+                stop=True,
+            )
+            return acc
+
+        x1 = pick("x1", l_offs, "x1_words")
+        x2 = pick("x2", l_two, "x2_words")
+        w1_q = quantise("w1q", round_weight("w1_bf", w1_raw, nc.scalar.copy), N)
+        x3 = pick("x3", l_three, "w1_bf")
+        w2_q = quantise("w2q", round_weight("w2_bf", w2_raw, nc.scalar.copy), N)
+
+        for t in range(PACK):
+            acc = product(w1_q, t, x1)
+            nc.scalar.activation(win_a[t][:, :N], acc[:], ACT.Copy, scale=ga_abs[:, t : t + 1])
+        w3_bf = round_weight("w3_bf", w3_raw, nc.scalar.copy)
+        for t in range(PACK):
+            acc = product(w2_q, t, x2)
+            nc.scalar.activation(win_b[t][:, :N], acc[:], ACT.Copy, scale=ga_abs[:, t : t + 1])
+
+        diff = []
+        near = []
+        for t in range(PACK + 1):
+            if t < PACK:
+                g = ring.tile([P, N], F32, name="y_n1")
+                nc.vector.tensor_copy(g[:], win_a[t][:].indirect(l_n1[:]))
+                near.append(g)
+            if t > 0:
+                dt = ring.tile([P, N], F32, name="diff")
+                nc.vector.scalar_tensor_tensor(dt[:], near[t - 1][:], -0.5, win_a[t - 1][:, :N], ALU.mult, ALU.add)
+                diff.append(dt)
+
+        w3_q = quantise("w3q", w3_bf, N)
+        b_abs = keep.tile([P, PACK, N], F32, name="b_abs", tag="chain", align_bytes=64)
+        b_g = keep.tile([P, PACK, N], F32, name="b_g")
+        for t in range(PACK):
+            acc = product(w3_q, t, x3)
+            nc.scalar.activation(b_abs[:, t, :], acc[:], ACT.Abs)
+            nc.scalar.activation(b_g[:, t, :], acc[:], ACT.Copy, scale=gb_sgn[:, t : t + 1])
+        for t in range(PACK):
+            nc.scalar.activation(win_a[t][:, :N], b_abs[:, t, :], ACT.Ln, bias=half[:])
+        inv = keep.tile([P, PACK, N], F32, name="inv", tag="chain", align_bytes=64)
+        for t in range(PACK):
+            nc.scalar.activation(inv[:, t, :], win_a[t][:].indirect(l_n4[:]), ACT.Exp, scale=-1.0)
+
+        low = keep.tile([P, PACK, N], F32, name="low")
+        d_n3 = keep.tile([P, PACK, N], F32, name="d_n3")
+        for t in range(PACK):
+            g = ring.tile([P, N], F32, name="d_n2")
+            nc.vector.tensor_copy(g[:], win_b[t][:].indirect(l_n2[:]))
+            nc.vector.tensor_copy(d_n3[:, t, :], win_b[t][:].indirect(l_n3[:]))
+            nc.vector.tensor_tensor(low[:, t, :], diff[t][:], g[:], ALU.min)
+
+        def clamp_half(h, z_bf):
+            cols = slice(2 * h, 2 * h + 2)
+            nc.vector.tensor_tensor(
+                z_bf[:].rearrange("p (e m k) -> p m k e", e=2, k=PACK),
+                low[:].rearrange("p k (m s) -> p m k s", s=PACK)[:, :, :, cols],
+                d_n3[:].rearrange("p k (m s) -> p m k s", s=PACK)[:, :, :, cols],
+                ALU.max,
+            )
+
+        z_lo = keep.tile([P, 2 * N], BF16, name="z_lo", align_bytes=64)
+        clamp_half(0, z_lo)
+        z_q = [quantise("zq0", z_lo, N // 2)]
+
+        z2_bf = keep.tile([P, PACK * N], BF16, name="z2_bf", align_bytes=64)
+        nc.vector.tensor_tensor(
+            z2_bf[:].rearrange("p (c i k) -> p c k i", i=4, k=PACK),
+            b_g[:].rearrange("p k (c i) -> p c k i", i=4),
+            inv[:].rearrange("p k (c i) -> p c k i", i=4),
+            ALU.mult,
+        )
+        z2_q = quantise("z2q", z2_bf, N)
+
+        z_hi = keep.tile([P, 2 * N], BF16, name="z_hi", tag="chain", align_bytes=64)
+        clamp_half(1, z_hi)
+        z_q.append(quantise("zq1", z_hi, N // 2))
+
+        out_rows = out.rearrange("(p t) v -> t p v", t=PACK)
+        for t in range(PACK):
+            acc = product(z_q[t // 2], t % 2, z2_q)
+            nc.scalar.activation(win_b[t][:, :N], acc[:], ACT.Copy, scale=0.0625)
+            g = ring.tile([P, N], F32, name="s_n6")
+            nc.vector.tensor_copy(g[:], win_b[t][:].indirect(l_n6[:]))
+            res = ring.tile([P, N], F32, name="res")
+            nc.vector.tensor_tensor(res[:], win_b[t][:].indirect(l_n5[:]), g[:], ALU.subtract)
+            nc.sync.dma_start(out_rows[t], res[:])

@@ -33,31 +33,31 @@ def tile_picked_twkclampbnormgap_none_p_kernel(
             nc.sync.dma_start(tile[:], src)
             return tile
 
-        def load_weight(name, src):
-            tile = keep.tile([P, PACK, N], F32, name=name)
-            nc.sync.dma_start(tile[:], src.rearrange("(p j) c -> p j c", j=PACK))
+        def load_half(name, src, h):
+            tile = keep.tile([P, PACK, N // 2], F32, name=name)
+            nc.sync.dma_start(tile[:], src.rearrange("(p j) c -> p j c", j=PACK)[:, :, h * N // 2 : (h + 1) * N // 2])
             return tile
 
         x_bytes = keep.tile([P, T], U8, name="x_bytes")
-        nc.vector.memset(x_bytes[:].bitcast(I32), 0)
+        nc.gpsimd.memset(x_bytes[:].bitcast(I32), 0)
+        for q in range(4):
+            nc.scalar.dma_start(
+                x_bytes[32 * q : 32 * q + 4, :].bitcast(I32), x_scales[0, 4 * q : 4 * q + 4, :].bitcast(I32)
+            )
         half = keep.tile([P, 1], F32, name="half")
-        nc.vector.memset(half[:], 0.5)
+        nc.gpsimd.memset(half[:], 0.5)
         warm = keep.tile([P, 1], F32, name="warm")
         nc.scalar.activation(warm[:], half[:], ACT.Ln)
 
         l_offs = load_list("l_offs", offs)
+        l_three = load_list("l_three", three)
         x_table = keep.tile([P, T], I32, name="x_table")
         nc.sync.dma_start(x_table[:], x_words[0].rearrange("p n t -> p (n t)").bitcast(I32))
-        for q in range(4):
-            nc.sync.dma_start(
-                x_bytes[32 * q : 32 * q + 4, :].bitcast(I32), x_scales[0, 4 * q : 4 * q + 4, :].bitcast(I32)
-            )
-        w1_raw = load_weight("w1_raw", w1)
+        w1_raw = [load_half("w1_raw%d" % h, w1, h) for h in range(2)]
         l_two = load_list("l_two", two)
-        l_three = load_list("l_three", three)
-        w2_raw = load_weight("w2_raw", w2)
+        w3_raw = [load_half("w3_raw%d" % h, w3, h) for h in range(2)]
         l_n1 = load_list("l_n1", n1)
-        w3_raw = load_weight("w3_raw", w3)
+        w2_raw = [load_half("w2_raw%d" % h, w2, h) for h in range(2)]
         l_n2 = load_list("l_n2", n2)
         l_n3 = load_list("l_n3", n3)
         l_n4 = load_list("l_n4", n4)
@@ -79,28 +79,36 @@ def tile_picked_twkclampbnormgap_none_p_kernel(
 
         win_a = [keep.tile([P, 2 * N], F32, name="win_a%d" % t) for t in range(PACK)]
         win_b = [keep.tile([P, 2 * N], F32, name="win_b%d" % t) for t in range(PACK)]
-        for win in win_a + win_b:
-            nc.vector.memset(win[:, N:], 0.0)
+        for t in range(PACK):
+            nc.vector.memset(win_a[t][:, N:], 0.0)
+            nc.gpsimd.memset(win_b[t][:, N:], 0.0)
 
-        def pick(name, offsets, tag):
-            words = keep.tile([P, N], U32, name=name + "_words", tag=tag, align_bytes=64)
-            scales = keep.tile([P, N], U8, name=name + "_scales", align_bytes=64)
+        def pick_words(name, offsets, tag):
+            words = keep.tile([P, N], U32, name=name, tag=tag, align_bytes=64)
             nc.vector.tensor_copy(words[:], x_table[:].bitcast(U32).indirect(offsets[:]))
-            nc.vector.tensor_copy(scales[:], x_bytes[:].indirect(offsets[:]))
-            return words, scales
+            return words
 
-        def quantise(name, rounded, width):
-            words = keep.tile([P, width], U32, name=name + "_words", align_bytes=64)
+        def pick_scales(name, offsets):
+            scales = keep.tile([P, N], U8, name=name, align_bytes=64)
+            nc.vector.tensor_copy(scales[:], x_bytes[:].indirect(offsets[:]))
+            return scales
+
+        def quantise(name, rounded, width, tag=None):
+            words = keep.tile([P, width], U32, name=name + "_words", tag=tag or name + "_words", align_bytes=64)
             scales = keep.tile([P, width], U8, name=name + "_scales", align_bytes=64)
             nc.vector.quantize_mx(out=words[:].bitcast(FP8X4), scales=scales[:], in_=rounded[:])
             return words, scales
 
-        def round_weight(name, raw, copy):
-            rounded = keep.tile([P, PACK * N], BF16, name=name, align_bytes=64)
+        def round_half(rounded, raw, h, copy):
             copy(
-                rounded[:].rearrange("p (t m j) -> p m j t", t=PACK, j=PACK),
-                raw[:].rearrange("p j (m t) -> p m j t", t=PACK),
+                rounded[:].rearrange("p (t m j) -> p m j t", t=PACK, j=PACK)[:, h * P // 2 : (h + 1) * P // 2],
+                raw[h][:].rearrange("p j (m t) -> p m j t", t=PACK),
             )
+
+        def round_weight(name, raw):
+            rounded = keep.tile([P, PACK * N], BF16, name=name, align_bytes=64)
+            for h in range(2):
+                round_half(rounded, raw, h, nc.scalar.copy)
             return rounded
 
         def product(stationary, tile_index, moving):
@@ -117,39 +125,49 @@ def tile_picked_twkclampbnormgap_none_p_kernel(
             )
             return acc
 
-        x1 = pick("x1", l_offs, "x1_words")
-        x2 = pick("x2", l_two, "x2_words")
-        w1_q = quantise("w1q", round_weight("w1_bf", w1_raw, nc.scalar.copy), N)
-        x3 = pick("x3", l_three, "w1_bf")
-        w2_q = quantise("w2q", round_weight("w2_bf", w2_raw, nc.scalar.copy), N)
+        x1_scales = pick_scales("x1_scales", l_offs)
+        x3_scales = pick_scales("x3_scales", l_three)
+        x1 = (pick_words("x1_words", l_offs, "x1_words"), x1_scales)
+        x3 = (pick_words("x3_words", l_three, "x3_words"), x3_scales)
+        x2_scales = pick_scales("x2_scales", l_two)
+        w1_q = quantise("w1q", round_weight("w1_bf", w1_raw), N)
+        x2 = (pick_words("x2_words", l_two, "w1_bf"), x2_scales)
+        w3_q = quantise("w3q", round_weight("w3_bf", w3_raw), N)
 
         for t in range(PACK):
             acc = product(w1_q, t, x1)
             nc.scalar.activation(win_a[t][:, :N], acc[:], ACT.Copy, scale=ga_abs[:, t : t + 1])
-        w3_bf = round_weight("w3_bf", w3_raw, nc.scalar.copy)
+        b_acc = [product(w3_q, t, x3) for t in range(PACK)]
+
+        def pull(dst, t):
+            nc.vector.tensor_scalar(dst, win_a[t][:].indirect(l_n1[:]), -0.5, 0.0, ALU.mult, ALU.add)
+
+        early = keep.tile([P, 3, N], F32, name="early")
+        rest = keep.tile([P, PACK - 1, N], F32, name="rest")
+        w2_bf = keep.tile([P, PACK * N], BF16, name="w2_bf", align_bytes=64)
+        pull(early[:, 0, :], 0)
+        round_half(w2_bf, w2_raw, 0, nc.vector.tensor_copy)
+        round_half(w2_bf, w2_raw, 1, nc.scalar.copy)
+        pull(early[:, 1, :], 1)
+        w2_q = quantise("w2q", w2_bf, N)
+        late = keep.tile([P, 2, N], F32, name="late", tag="w2_bf", align_bytes=64)
+        pull(late[:, 1, :], 2)
+        pull(early[:, 2, :], 3)
+        near = [early[:, 0, :], early[:, 1, :], late[:, 1, :], early[:, 2, :]]
+        diff = [late[:, 0, :]] + [rest[:, t, :] for t in range(PACK - 1)]
+        for t in range(PACK):
+            nc.gpsimd.tensor_tensor(diff[t], near[t], win_a[t][:, :N], ALU.add)
+
         for t in range(PACK):
             acc = product(w2_q, t, x2)
             nc.scalar.activation(win_b[t][:, :N], acc[:], ACT.Copy, scale=ga_abs[:, t : t + 1])
 
-        diff = []
-        near = []
-        for t in range(PACK + 1):
-            if t < PACK:
-                g = ring.tile([P, N], F32, name="y_n1")
-                nc.vector.tensor_copy(g[:], win_a[t][:].indirect(l_n1[:]))
-                near.append(g)
-            if t > 0:
-                dt = ring.tile([P, N], F32, name="diff")
-                nc.vector.scalar_tensor_tensor(dt[:], near[t - 1][:], -0.5, win_a[t - 1][:, :N], ALU.mult, ALU.add)
-                diff.append(dt)
-
-        w3_q = quantise("w3q", w3_bf, N)
         b_abs = keep.tile([P, PACK, N], F32, name="b_abs", tag="chain", align_bytes=64)
-        b_g = keep.tile([P, PACK, N], F32, name="b_g")
+        b_g = keep.tile([P, PACK, N], F32, name="b_g", align_bytes=64)
         for t in range(PACK):
-            acc = product(w3_q, t, x3)
-            nc.scalar.activation(b_abs[:, t, :], acc[:], ACT.Abs)
-            nc.scalar.activation(b_g[:, t, :], acc[:], ACT.Copy, scale=gb_sgn[:, t : t + 1])
+            nc.scalar.activation(b_abs[:, t, :], b_acc[t][:], ACT.Abs)
+        for t in range(PACK):
+            nc.scalar.activation(b_g[:, t, :], b_acc[t][:], ACT.Copy, scale=gb_sgn[:, t : t + 1])
         for t in range(PACK):
             nc.scalar.activation(win_a[t][:, :N], b_abs[:, t, :], ACT.Ln, bias=half[:])
         inv = keep.tile([P, PACK, N], F32, name="inv", tag="chain", align_bytes=64)
@@ -157,12 +175,13 @@ def tile_picked_twkclampbnormgap_none_p_kernel(
             nc.scalar.activation(inv[:, t, :], win_a[t][:].indirect(l_n4[:]), ACT.Exp, scale=-1.0)
 
         low = keep.tile([P, PACK, N], F32, name="low")
+        d_n2 = keep.tile([P, PACK, N], F32, name="d_n2")
         d_n3 = keep.tile([P, PACK, N], F32, name="d_n3")
         for t in range(PACK):
-            g = ring.tile([P, N], F32, name="d_n2")
-            nc.vector.tensor_copy(g[:], win_b[t][:].indirect(l_n2[:]))
+            nc.vector.tensor_copy(d_n2[:, t, :], win_b[t][:].indirect(l_n2[:]))
+        for t in range(PACK):
             nc.vector.tensor_copy(d_n3[:, t, :], win_b[t][:].indirect(l_n3[:]))
-            nc.vector.tensor_tensor(low[:, t, :], diff[t][:], g[:], ALU.min)
+            nc.vector.tensor_tensor(low[:, t, :], diff[t], d_n2[:, t, :], ALU.min)
 
         def clamp_half(h, z_bf):
             cols = slice(2 * h, 2 * h + 2)
@@ -175,7 +194,6 @@ def tile_picked_twkclampbnormgap_none_p_kernel(
 
         z_lo = keep.tile([P, 2 * N], BF16, name="z_lo", align_bytes=64)
         clamp_half(0, z_lo)
-        z_q = [quantise("zq0", z_lo, N // 2)]
 
         z2_bf = keep.tile([P, PACK * N], BF16, name="z2_bf", align_bytes=64)
         nc.vector.tensor_tensor(
@@ -184,6 +202,7 @@ def tile_picked_twkclampbnormgap_none_p_kernel(
             inv[:].rearrange("p k (c i) -> p c k i", i=4),
             ALU.mult,
         )
+        z_q = [quantise("zq0", z_lo, N // 2, "b_g")]
         z2_q = quantise("z2q", z2_bf, N)
 
         z_hi = keep.tile([P, 2 * N], BF16, name="z_hi", tag="chain", align_bytes=64)
@@ -191,11 +210,19 @@ def tile_picked_twkclampbnormgap_none_p_kernel(
         z_q.append(quantise("zq1", z_hi, N // 2))
 
         out_rows = out.rearrange("(p t) v -> t p v", t=PACK)
-        for t in range(PACK):
-            acc = product(z_q[t // 2], t % 2, z2_q)
-            nc.scalar.activation(win_b[t][:, :N], acc[:], ACT.Copy, scale=0.0625)
-            g = ring.tile([P, N], F32, name="s_n6")
-            nc.vector.tensor_copy(g[:], win_b[t][:].indirect(l_n6[:]))
-            res = ring.tile([P, N], F32, name="res")
-            nc.vector.tensor_tensor(res[:], win_b[t][:].indirect(l_n5[:]), g[:], ALU.subtract)
-            nc.sync.dma_start(out_rows[t], res[:])
+        s_n6 = keep.tile([P, PACK, N], F32, name="s_n6")
+        for t in range(PACK + 1):
+            if t < PACK:
+                acc = product(z_q[t // 2], t % 2, z2_q)
+                nc.scalar.activation(win_b[t][:, :N], acc[:], ACT.Copy, scale=0.0625)
+                nc.vector.tensor_copy(s_n6[:, t, :], win_b[t][:].indirect(l_n6[:]))
+            if t > 0:
+                u = t - 1
+                pieces = 2 if u == PACK - 1 else 1
+                width = N // pieces
+                for c in range(pieces):
+                    cols = slice(c * width, (c + 1) * width)
+                    res = ring.tile([P, width], F32, name="res")
+                    offsets = l_n5[:, c * width // 16 : (c + 1) * width // 16]
+                    nc.vector.tensor_tensor(res[:], win_b[u][:].indirect(offsets), s_n6[:, u, cols], ALU.subtract)
+                    nc.sync.dma_start(out_rows[u][:, cols], res[:])

@@ -16,6 +16,7 @@ P = 128
 T = 2048
 N = 512
 PACK = 4
+SPLIT = 64
 FLOPS = 4 * 2 * 512 * 512 * 512
 
 
@@ -34,30 +35,31 @@ def tile_picked_twkclampbnormgap_none_p_kernel(
             return tile
 
         def load_half(name, src, h):
-            tile = keep.tile([P, PACK, N // 2], F32, name=name)
+            tile = keep.tile([P, PACK, N // 2], F32, name=name, align_bytes=64)
             nc.sync.dma_start(tile[:], src.rearrange("(p j) c -> p j c", j=PACK)[:, :, h * N // 2 : (h + 1) * N // 2])
             return tile
 
         x_bytes = keep.tile([P, T], U8, name="x_bytes")
-        nc.gpsimd.memset(x_bytes[:].bitcast(I32), 0)
-        for q in range(4):
-            nc.scalar.dma_start(
-                x_bytes[32 * q : 32 * q + 4, :].bitcast(I32), x_scales[0, 4 * q : 4 * q + 4, :].bitcast(I32)
-            )
+        nc.vector.memset(x_bytes[:].bitcast(I32), 0)
         half = keep.tile([P, 1], F32, name="half")
-        nc.gpsimd.memset(half[:], 0.5)
+        nc.vector.memset(half[:], 0.5)
         warm = keep.tile([P, 1], F32, name="warm")
         nc.scalar.activation(warm[:], half[:], ACT.Ln)
 
-        l_offs = load_list("l_offs", offs)
-        l_three = load_list("l_three", three)
         x_table = keep.tile([P, T], I32, name="x_table")
         nc.sync.dma_start(x_table[:], x_words[0].rearrange("p n t -> p (n t)").bitcast(I32))
+        l_offs = load_list("l_offs", offs)
+        for q in range(4):
+            nc.sync.dma_start(
+                x_bytes[32 * q : 32 * q + 4, :].bitcast(I32), x_scales[0, 4 * q : 4 * q + 4, :].bitcast(I32)
+            )
         w1_raw = [load_half("w1_raw%d" % h, w1, h) for h in range(2)]
+        l_three = load_list("l_three", three)
         l_two = load_list("l_two", two)
         w3_raw = [load_half("w3_raw%d" % h, w3, h) for h in range(2)]
         l_n1 = load_list("l_n1", n1)
-        w2_raw = [load_half("w2_raw%d" % h, w2, h) for h in range(2)]
+        w2_raw = keep.tile([P, PACK, N], F32, name="w2_raw")
+        nc.sync.dma_start(w2_raw[:], w2.rearrange("(p j) c -> p j c", j=PACK))
         l_n2 = load_list("l_n2", n2)
         l_n3 = load_list("l_n3", n3)
         l_n4 = load_list("l_n4", n4)
@@ -70,11 +72,9 @@ def tile_picked_twkclampbnormgap_none_p_kernel(
         nc.gpsimd.dma_start(gb_t[:], gb.rearrange("(p t) o -> p (t o)", t=PACK))
         step = keep.tile([P, PACK], F32, name="step")
         sgn = keep.tile([P, PACK], F32, name="sgn")
-        ga_abs = keep.tile([P, PACK], F32, name="ga_abs")
         gb_sgn = keep.tile([P, PACK], F32, name="gb_sgn")
         nc.gpsimd.tensor_scalar(step[:], ga_t[:], 0.0, 2.0, ALU.is_ge, ALU.mult)
         nc.gpsimd.tensor_scalar(sgn[:], step[:], 1.0, -1.0, ALU.mult, ALU.add)
-        nc.gpsimd.tensor_tensor(ga_abs[:], ga_t[:], sgn[:], ALU.mult)
         nc.gpsimd.tensor_tensor(gb_sgn[:], gb_t[:], sgn[:], ALU.mult)
 
         win_a = [keep.tile([P, 2 * N], F32, name="win_a%d" % t) for t in range(PACK)]
@@ -88,8 +88,8 @@ def tile_picked_twkclampbnormgap_none_p_kernel(
             nc.vector.tensor_copy(words[:], x_table[:].bitcast(U32).indirect(offsets[:]))
             return words
 
-        def pick_scales(name, offsets):
-            scales = keep.tile([P, N], U8, name=name, align_bytes=64)
+        def pick_scales(name, offsets, tag):
+            scales = keep.tile([P, N], U8, name=name, tag=tag, align_bytes=64)
             nc.vector.tensor_copy(scales[:], x_bytes[:].indirect(offsets[:]))
             return scales
 
@@ -99,16 +99,16 @@ def tile_picked_twkclampbnormgap_none_p_kernel(
             nc.vector.quantize_mx(out=words[:].bitcast(FP8X4), scales=scales[:], in_=rounded[:])
             return words, scales
 
-        def round_half(rounded, raw, h, copy):
+        def round_part(rounded, m0, m1, raw, copy):
             copy(
-                rounded[:].rearrange("p (t m j) -> p m j t", t=PACK, j=PACK)[:, h * P // 2 : (h + 1) * P // 2],
-                raw[h][:].rearrange("p j (m t) -> p m j t", t=PACK),
+                rounded[:].rearrange("p (t m j) -> p m j t", t=PACK, j=PACK)[:, m0:m1],
+                raw.rearrange("p j (m t) -> p m j t", t=PACK),
             )
 
         def round_weight(name, raw):
             rounded = keep.tile([P, PACK * N], BF16, name=name, align_bytes=64)
             for h in range(2):
-                round_half(rounded, raw, h, nc.scalar.copy)
+                round_part(rounded, h * P // 2, (h + 1) * P // 2, raw[h][:], nc.scalar.copy)
             return rounded
 
         def product(stationary, tile_index, moving):
@@ -125,14 +125,15 @@ def tile_picked_twkclampbnormgap_none_p_kernel(
             )
             return acc
 
-        x1_scales = pick_scales("x1_scales", l_offs)
-        x3_scales = pick_scales("x3_scales", l_three)
-        x1 = (pick_words("x1_words", l_offs, "x1_words"), x1_scales)
-        x3 = (pick_words("x3_words", l_three, "x3_words"), x3_scales)
-        x2_scales = pick_scales("x2_scales", l_two)
+        x1 = (pick_words("x1_words", l_offs, "x1_words"), pick_scales("x1_scales", l_offs, "x1_scales"))
+        x3_words = pick_words("x3_words", l_three, "x3_words")
         w1_q = quantise("w1q", round_weight("w1_bf", w1_raw), N)
-        x2 = (pick_words("x2_words", l_two, "w1_bf"), x2_scales)
+        x3 = (x3_words, pick_scales("x3_scales", l_three, "w1_raw1"))
+        x2_words = pick_words("x2_words", l_two, "w1_bf")
         w3_q = quantise("w3q", round_weight("w3_bf", w3_raw), N)
+        x2 = (x2_words, pick_scales("x2_scales", l_two, "w3_bf"))
+        ga_abs = keep.tile([P, PACK], F32, name="ga_abs", tag="w3_raw1", align_bytes=64)
+        nc.scalar.activation(ga_abs[:], ga_t[:], ACT.Abs)
 
         for t in range(PACK):
             acc = product(w1_q, t, x1)
@@ -142,25 +143,20 @@ def tile_picked_twkclampbnormgap_none_p_kernel(
         def pull(dst, t):
             nc.vector.tensor_scalar(dst, win_a[t][:].indirect(l_n1[:]), -0.5, 0.0, ALU.mult, ALU.add)
 
-        early = keep.tile([P, 3, N], F32, name="early")
-        rest = keep.tile([P, PACK - 1, N], F32, name="rest")
         w2_bf = keep.tile([P, PACK * N], BF16, name="w2_bf", align_bytes=64)
-        pull(early[:, 0, :], 0)
-        round_half(w2_bf, w2_raw, 0, nc.vector.tensor_copy)
-        round_half(w2_bf, w2_raw, 1, nc.scalar.copy)
-        pull(early[:, 1, :], 1)
+        round_part(w2_bf, 0, SPLIT, w2_raw[:, :, : PACK * SPLIT], nc.vector.tensor_copy)
+        round_part(w2_bf, SPLIT, P, w2_raw[:, :, PACK * SPLIT :], nc.scalar.copy)
+        early = keep.tile([P, N], F32, name="early")
+        pull(early[:], 0)
         w2_q = quantise("w2q", w2_bf, N)
-        late = keep.tile([P, 2, N], F32, name="late", tag="w2_bf", align_bytes=64)
-        pull(late[:, 1, :], 2)
-        pull(early[:, 2, :], 3)
-        near = [early[:, 0, :], early[:, 1, :], late[:, 1, :], early[:, 2, :]]
+        late = keep.tile([P, PACK, N], F32, name="late", tag="w2_bf", align_bytes=64)
+        rest = keep.tile([P, PACK - 1, N], F32, name="rest")
+        for t in range(1, PACK):
+            pull(late[:, t, :], t)
+        near = [early[:]] + [late[:, t, :] for t in range(1, PACK)]
         diff = [late[:, 0, :]] + [rest[:, t, :] for t in range(PACK - 1)]
         for t in range(PACK):
             nc.gpsimd.tensor_tensor(diff[t], near[t], win_a[t][:, :N], ALU.add)
-
-        for t in range(PACK):
-            acc = product(w2_q, t, x2)
-            nc.scalar.activation(win_b[t][:, :N], acc[:], ACT.Copy, scale=ga_abs[:, t : t + 1])
 
         b_abs = keep.tile([P, PACK, N], F32, name="b_abs", tag="chain", align_bytes=64)
         b_g = keep.tile([P, PACK, N], F32, name="b_g", align_bytes=64)
@@ -168,6 +164,9 @@ def tile_picked_twkclampbnormgap_none_p_kernel(
             nc.scalar.activation(b_abs[:, t, :], b_acc[t][:], ACT.Abs)
         for t in range(PACK):
             nc.scalar.activation(b_g[:, t, :], b_acc[t][:], ACT.Copy, scale=gb_sgn[:, t : t + 1])
+        for t in range(PACK):
+            acc = product(w2_q, t, x2)
+            nc.scalar.activation(win_b[t][:, :N], acc[:], ACT.Copy, scale=ga_abs[:, t : t + 1])
         for t in range(PACK):
             nc.scalar.activation(win_a[t][:, :N], b_abs[:, t, :], ACT.Ln, bias=half[:])
         inv = keep.tile([P, PACK, N], F32, name="inv", tag="chain", align_bytes=64)
@@ -210,7 +209,7 @@ def tile_picked_twkclampbnormgap_none_p_kernel(
         z_q.append(quantise("zq1", z_hi, N // 2))
 
         out_rows = out.rearrange("(p t) v -> t p v", t=PACK)
-        s_n6 = keep.tile([P, PACK, N], F32, name="s_n6")
+        s_n6 = keep.tile([P, PACK, N], F32, name="s_n6", tag="chain", align_bytes=64)
         for t in range(PACK + 1):
             if t < PACK:
                 acc = product(z_q[t // 2], t % 2, z2_q)
@@ -222,7 +221,7 @@ def tile_picked_twkclampbnormgap_none_p_kernel(
                 width = N // pieces
                 for c in range(pieces):
                     cols = slice(c * width, (c + 1) * width)
-                    res = ring.tile([P, width], F32, name="res")
+                    res = ring.tile([P, width], F32, name="res")[:]
                     offsets = l_n5[:, c * width // 16 : (c + 1) * width // 16]
-                    nc.vector.tensor_tensor(res[:], win_b[u][:].indirect(offsets), s_n6[:, u, cols], ALU.subtract)
-                    nc.sync.dma_start(out_rows[u][:, cols], res[:])
+                    nc.vector.tensor_tensor(res, win_b[u][:].indirect(offsets), s_n6[:, u, cols], ALU.subtract)
+                    nc.sync.dma_start(out_rows[u][:, cols], res)

from contextlib import ExitStack

import concourse.mybir as mybir

F32 = mybir.dt.float32
BF16 = mybir.dt.bfloat16
I32 = mybir.dt.int32
U32 = mybir.dt.uint32
U16 = mybir.dt.uint16
U8 = mybir.dt.uint8
FP8X4 = mybir.dt.float8_e4m3fn_x4
ALU = mybir.AluOpType
ACT = mybir.ActivationFunctionType

P = 128
T = 2048
N = 512
PACK = 4
SPLIT = 64
FLOPS = 4 * 2 * 512 * 512 * 512


def tile_picked_twkclampbnormgap_none_p_kernel(
    tc, x_words, x_scales, w1, w2, w3, ga, gb, offs, two, n1, n2, n3, three, n4, n5, n6, out
):
    nc = tc.nc
    with ExitStack() as ctx:
        keep = ctx.enter_context(tc.tile_pool(name="keep", bufs=1))
        ring = ctx.enter_context(tc.tile_pool(name="ring", bufs=4))
        psum = ctx.enter_context(tc.psum_pool(name="psum", bufs=8))

        def load_list(name, src):
            tile = keep.tile([P, N // 16], U16, name=name)
            nc.sync.dma_start(tile[:], src)
            return tile

        def load_half(name, src, h):
            tile = keep.tile([P, PACK, N // 2], F32, name=name, align_bytes=64)
            nc.sync.dma_start(tile[:], src.rearrange("(p j) c -> p j c", j=PACK)[:, :, h * N // 2 : (h + 1) * N // 2])
            return tile

        x_bytes = keep.tile([P, T], U8, name="x_bytes")
        nc.vector.memset(x_bytes[:].bitcast(I32), 0)
        half = keep.tile([P, 1], F32, name="half")
        nc.vector.memset(half[:], 0.5)
        warm = keep.tile([P, 1], F32, name="warm")
        nc.scalar.activation(warm[:], half[:], ACT.Ln)

        x_table = keep.tile([P, T], I32, name="x_table")
        nc.sync.dma_start(x_table[:], x_words[0].rearrange("p n t -> p (n t)").bitcast(I32))
        l_offs = load_list("l_offs", offs)
        for q in range(4):
            nc.sync.dma_start(
                x_bytes[32 * q : 32 * q + 4, :].bitcast(I32), x_scales[0, 4 * q : 4 * q + 4, :].bitcast(I32)
            )
        w1_raw = [load_half("w1_raw%d" % h, w1, h) for h in range(2)]
        l_three = load_list("l_three", three)
        l_two = load_list("l_two", two)
        w3_raw = [load_half("w3_raw%d" % h, w3, h) for h in range(2)]
        l_n1 = load_list("l_n1", n1)
        w2_raw = keep.tile([P, PACK, N], F32, name="w2_raw")
        nc.sync.dma_start(w2_raw[:], w2.rearrange("(p j) c -> p j c", j=PACK))
        l_n2 = load_list("l_n2", n2)
        l_n3 = load_list("l_n3", n3)
        l_n4 = load_list("l_n4", n4)
        l_n6 = load_list("l_n6", n6)
        l_n5 = load_list("l_n5", n5)

        ga_t = keep.tile([P, PACK], F32, name="ga_t")
        gb_t = keep.tile([P, PACK], F32, name="gb_t")
        nc.gpsimd.dma_start(ga_t[:], ga.rearrange("(p t) o -> p (t o)", t=PACK))
        nc.gpsimd.dma_start(gb_t[:], gb.rearrange("(p t) o -> p (t o)", t=PACK))
        step = keep.tile([P, PACK], F32, name="step")
        sgn = keep.tile([P, PACK], F32, name="sgn")
        gb_sgn = keep.tile([P, PACK], F32, name="gb_sgn")
        nc.gpsimd.tensor_scalar(step[:], ga_t[:], 0.0, 2.0, ALU.is_ge, ALU.mult)
        nc.gpsimd.tensor_scalar(sgn[:], step[:], 1.0, -1.0, ALU.mult, ALU.add)
        nc.gpsimd.tensor_tensor(gb_sgn[:], gb_t[:], sgn[:], ALU.mult)

        win_a = [keep.tile([P, 2 * N], F32, name="win_a%d" % t) for t in range(PACK)]
        win_b = [keep.tile([P, 2 * N], F32, name="win_b%d" % t) for t in range(PACK)]
        for t in range(PACK):
            nc.vector.memset(win_a[t][:, N:], 0.0)
            nc.gpsimd.memset(win_b[t][:, N:], 0.0)

        def pick_words(name, offsets, tag):
            words = keep.tile([P, N], U32, name=name, tag=tag, align_bytes=64)
            nc.vector.tensor_copy(words[:], x_table[:].bitcast(U32).indirect(offsets[:]))
            return words

        def pick_scales(name, offsets, tag):
            scales = keep.tile([P, N], U8, name=name, tag=tag, align_bytes=64)
            nc.vector.tensor_copy(scales[:], x_bytes[:].indirect(offsets[:]))
            return scales

        def quantise(name, rounded, width, tag=None):
            words = keep.tile([P, width], U32, name=name + "_words", tag=tag or name + "_words", align_bytes=64)
            scales = keep.tile([P, width], U8, name=name + "_scales", align_bytes=64)
            nc.vector.quantize_mx(out=words[:].bitcast(FP8X4), scales=scales[:], in_=rounded[:])
            return words, scales

        def round_part(rounded, m0, m1, raw, copy):
            copy(
                rounded[:].rearrange("p (t m j) -> p m j t", t=PACK, j=PACK)[:, m0:m1],
                raw.rearrange("p j (m t) -> p m j t", t=PACK),
            )

        def round_weight(name, raw):
            rounded = keep.tile([P, PACK * N], BF16, name=name, align_bytes=64)
            for h in range(2):
                round_part(rounded, h * P // 2, (h + 1) * P // 2, raw[h][:], nc.scalar.copy)
            return rounded

        def product(stationary, tile_index, moving):
            acc = psum.tile([P, N], F32, name="acc")
            cols = slice(tile_index * P, (tile_index + 1) * P)
            nc.tensor.matmul_mx(
                out=acc[:],
                lhsT=stationary[0][:, cols].bitcast(FP8X4),
                lhsT_scale=stationary[1][:, cols],
                rhs=moving[0][:].bitcast(FP8X4),
                rhs_scale=moving[1][:],
                start=True,
                stop=True,
            )
            return acc

        x1 = (pick_words("x1_words", l_offs, "x1_words"), pick_scales("x1_scales", l_offs, "x1_scales"))
        x3_words = pick_words("x3_words", l_three, "x3_words")
        w1_q = quantise("w1q", round_weight("w1_bf", w1_raw), N)
        x3 = (x3_words, pick_scales("x3_scales", l_three, "w1_raw1"))
        x2_words = pick_words("x2_words", l_two, "w1_bf")
        w3_q = quantise("w3q", round_weight("w3_bf", w3_raw), N)
        x2 = (x2_words, pick_scales("x2_scales", l_two, "w3_bf"))
        ga_abs = keep.tile([P, PACK], F32, name="ga_abs", tag="w3_raw1", align_bytes=64)
        nc.scalar.activation(ga_abs[:], ga_t[:], ACT.Abs)

        for t in range(PACK):
            acc = product(w1_q, t, x1)
            nc.scalar.activation(win_a[t][:, :N], acc[:], ACT.Copy, scale=ga_abs[:, t : t + 1])
        b_acc = [product(w3_q, t, x3) for t in range(PACK)]

        def pull(dst, t):
            nc.vector.tensor_scalar(dst, win_a[t][:].indirect(l_n1[:]), -0.5, 0.0, ALU.mult, ALU.add)

        w2_bf = keep.tile([P, PACK * N], BF16, name="w2_bf", align_bytes=64)
        round_part(w2_bf, 0, SPLIT, w2_raw[:, :, : PACK * SPLIT], nc.vector.tensor_copy)
        round_part(w2_bf, SPLIT, P, w2_raw[:, :, PACK * SPLIT :], nc.scalar.copy)
        early = keep.tile([P, N], F32, name="early")
        pull(early[:], 0)
        w2_q = quantise("w2q", w2_bf, N)
        late = keep.tile([P, PACK, N], F32, name="late", tag="w2_bf", align_bytes=64)
        rest = keep.tile([P, PACK - 1, N], F32, name="rest")
        for t in range(1, PACK):
            pull(late[:, t, :], t)
        near = [early[:]] + [late[:, t, :] for t in range(1, PACK)]
        diff = [late[:, 0, :]] + [rest[:, t, :] for t in range(PACK - 1)]
        for t in range(PACK):
            nc.gpsimd.tensor_tensor(diff[t], near[t], win_a[t][:, :N], ALU.add)

        b_abs = keep.tile([P, PACK, N], F32, name="b_abs", tag="chain", align_bytes=64)
        b_g = keep.tile([P, PACK, N], F32, name="b_g", align_bytes=64)
        for t in range(PACK):
            nc.scalar.activation(b_abs[:, t, :], b_acc[t][:], ACT.Abs)
        for t in range(PACK):
            nc.scalar.activation(b_g[:, t, :], b_acc[t][:], ACT.Copy, scale=gb_sgn[:, t : t + 1])
        for t in range(PACK):
            acc = product(w2_q, t, x2)
            nc.scalar.activation(win_b[t][:, :N], acc[:], ACT.Copy, scale=ga_abs[:, t : t + 1])
        for t in range(PACK):
            nc.scalar.activation(win_a[t][:, :N], b_abs[:, t, :], ACT.Ln, bias=half[:])
        inv = keep.tile([P, PACK, N], F32, name="inv", tag="chain", align_bytes=64)
        for t in range(PACK):
            nc.scalar.activation(inv[:, t, :], win_a[t][:].indirect(l_n4[:]), ACT.Exp, scale=-1.0)

        low = keep.tile([P, PACK, N], F32, name="low")
        d_n2 = keep.tile([P, PACK, N], F32, name="d_n2")
        d_n3 = keep.tile([P, PACK, N], F32, name="d_n3")
        for t in range(PACK):
            nc.vector.tensor_copy(d_n2[:, t, :], win_b[t][:].indirect(l_n2[:]))
        for t in range(PACK):
            nc.vector.tensor_copy(d_n3[:, t, :], win_b[t][:].indirect(l_n3[:]))
            nc.vector.tensor_tensor(low[:, t, :], diff[t], d_n2[:, t, :], ALU.min)

        def clamp_half(h, z_bf):
            cols = slice(2 * h, 2 * h + 2)
            nc.vector.tensor_tensor(
                z_bf[:].rearrange("p (e m k) -> p m k e", e=2, k=PACK),
                low[:].rearrange("p k (m s) -> p m k s", s=PACK)[:, :, :, cols],
                d_n3[:].rearrange("p k (m s) -> p m k s", s=PACK)[:, :, :, cols],
                ALU.max,
            )

        z_lo = keep.tile([P, 2 * N], BF16, name="z_lo", align_bytes=64)
        clamp_half(0, z_lo)

        z2_bf = keep.tile([P, PACK * N], BF16, name="z2_bf", align_bytes=64)
        nc.vector.tensor_tensor(
            z2_bf[:].rearrange("p (c i k) -> p c k i", i=4, k=PACK),
            b_g[:].rearrange("p k (c i) -> p c k i", i=4),
            inv[:].rearrange("p k (c i) -> p c k i", i=4),
            ALU.mult,
        )
        z_q = [quantise("zq0", z_lo, N // 2, "b_g")]
        z2_q = quantise("z2q", z2_bf, N)

        z_hi = keep.tile([P, 2 * N], BF16, name="z_hi", tag="chain", align_bytes=64)
        clamp_half(1, z_hi)
        z_q.append(quantise("zq1", z_hi, N // 2))

        out_rows = out.rearrange("(p t) v -> t p v", t=PACK)
        s_n6 = keep.tile([P, PACK, N], F32, name="s_n6", tag="chain", align_bytes=64)
        for t in range(PACK + 1):
            if t < PACK:
                acc = product(z_q[t // 2], t % 2, z2_q)
                nc.scalar.activation(win_b[t][:, :N], acc[:], ACT.Copy, scale=0.0625)
                nc.vector.tensor_copy(s_n6[:, t, :], win_b[t][:].indirect(l_n6[:]))
            if t > 0:
                u = t - 1
                pieces = 2 if u == PACK - 1 else 1
                width = N // pieces
                for c in range(pieces):
                    cols = slice(c * width, (c + 1) * width)
                    res = ring.tile([P, width], F32, name="res")[:]
                    offsets = l_n5[:, c * width // 16 : (c + 1) * width // 16]
                    nc.vector.tensor_tensor(res, win_b[u][:].indirect(offsets), s_n6[:, u, cols], ALU.subtract)
                    nc.sync.dma_start(out_rows[u][:, cols], res)
